import numpy as np
import ml_dtypes


def mxq(x, axis, fmt="e4m3"):
    dtype, down = {"e4m3": (ml_dtypes.float8_e4m3fn, 7), "e5m2": (ml_dtypes.float8_e5m2, 14)}[fmt]
    v = np.moveaxis(np.asarray(x, np.float32).astype(ml_dtypes.bfloat16).astype(np.float64), axis, -1)
    blocks = v.reshape(v.shape[:-1] + (-1, 32))
    amax = np.abs(blocks).max(-1, keepdims=True)
    byte = np.maximum(np.where(amax > 0, np.frexp(amax)[1] - 1 + 127, 0) - down, 1)
    scale = np.exp2(byte - 127.0)
    codes = (blocks / scale).astype(np.float32).astype(dtype).astype(np.float64)
    return np.moveaxis((codes * scale).reshape(v.shape), -1, axis)


WIDE = False


def mx_kscale(k):
    if not WIDE:
        return np.ones(k)
    levels = np.array([10, -10, 5, -5, 0])
    if k % 512:
        return np.exp2(np.random.permutation(np.resize(levels, k // 32))).repeat(32)
    a = np.empty((k // 512, 16))
    for p in range(k // 512):
        a[p, :8] = np.random.permutation(np.resize(levels, 8))
        for g in range(8):
            far = levels[np.abs(levels - a[p, g]) >= 10]
            a[p, g + 8] = far[np.random.randint(len(far))]
    return np.exp2(a.ravel()).repeat(32)


def f64(x):
    return np.asarray(x).astype(np.float64)


def striped(idx):
    return np.tile(idx.reshape(-1, 16).T, (8, 1)).astype(np.uint16)


def unstriped(offs):
    return offs[:16].T.reshape(-1).astype(np.int64)


def pack_weight(w):
    k, n = w.shape
    w = f64(np.asarray(w, np.float32).astype(ml_dtypes.bfloat16)).reshape(k // 32, 32, n)
    amax = np.abs(w).max(1)
    byte = np.clip(np.where(amax > 0, np.frexp(amax)[1] - 1 + 127 - 7, 1), 1, 254)
    scaled = (w * np.exp2(127.0 - byte)[:, None, :]).reshape(k, n).astype(np.float32)
    words = np.ascontiguousarray(scaled.reshape(k // 512, 128, 4, n).transpose(0, 1, 3, 2)).astype(ml_dtypes.float8_e4m3fn).view(np.uint8)
    return words, np.ascontiguousarray(byte.astype(np.uint8).reshape(k // 512, 16, n))


def unpack_weight(words, scales):
    g, p, n, _ = words.shape
    vals = np.ascontiguousarray(words).view(ml_dtypes.float8_e4m3fn).astype(np.float64) * np.repeat(np.exp2(scales.astype(np.float64) - 127.0), 8, axis=1)[..., None]
    return vals.transpose(0, 1, 3, 2).reshape(g * 512, n)


def gelu(v):
    return 0.5 * v * (1.0 + np.tanh(np.sqrt(2.0 / np.pi) * (v + 0.044715 * v**3)))


K, T, E, C, N = 2560, 768, 12, 256, 128
TOP = 4


def by_expert(wq, xq):
    return np.concatenate([wq[e].T @ xq[:, e * C:(e + 1) * C] for e in range(E)], axis=1)


def setup_inputs():
    n = np.random.standard_normal
    s = mx_kscale(K)[:, None]
    deal = np.repeat(np.arange(E), C).reshape(TOP, T)[:, np.random.permutation(T)]
    deal = np.take_along_axis(deal, np.argsort(np.random.rand(TOP, T), axis=0), axis=0)
    for _ in range(8):
        s_, t_ = np.random.permutation(T).reshape(2, -1); r = np.random.randint(TOP, size=T // 2); x, y = deal[r, s_].copy(), deal[r, t_].copy()
        ok = ~((deal[:, s_] == y).any(0) | (deal[:, t_] == x).any(0)); deal[r[ok], s_[ok]] = y[ok]; deal[r[ok], t_[ok]] = x[ok]
    order = np.lexsort((np.random.rand(TOP * T), deal.reshape(-1)))
    slot_token = order % T; pos = np.empty(TOP * T, np.int64); pos[order] = np.arange(TOP * T); pos = pos.reshape(TOP, T)
    g = np.random.uniform(0.5, 1.5, (TOP, T)); g = g / g.sum(0)
    packed = [pack_weight(m) for m in n((E, K, N)) / np.sqrt(K) / s[None]]
    w_slot = np.empty(E * C)
    for r in range(TOP): w_slot[pos[r]] = g[r]
    return {
        "xT": (n((K, T)) * s).astype(np.float32),
        "w_words": np.stack([m[0] for m in packed]),
        "w_scales": np.stack([m[1] for m in packed]),
        "b": (0.3 * n((N, E))).astype(np.float32),
        "gate": np.tile(w_slot, (K, 1)).astype(np.float32),
        "offs": striped(slot_token),
        "pos1": striped(pos[0]),
        "pos2": striped(pos[1]),
        "pos3": striped(pos[2]),
        "pos4": striped(pos[3]),
    }


def reference(xT, w_words, w_scales, b, gate, offs, pos1, pos2, pos3, pos4):
    idx = unstriped(offs)
    w = np.stack([unpack_weight(w_words[e], w_scales[e]) for e in range(E)])
    xq = mxq(f64(gate) * f64(xT)[:, idx], 0, "e4m3")
    y = by_expert(w, xq)
    y = gelu(y + np.repeat(f64(b), C, axis=1))
    return y[:, unstriped(pos1)] + y[:, unstriped(pos2)] + y[:, unstriped(pos3)] + y[:, unstriped(pos4)]

from contextlib import ExitStack

import concourse.mybir as mybir

K, T, E, C, N = 2560, 768, 12, 256, 128
S = E * C
P = 128
PACK = 4
PASSES = K // (P * PACK)
CHUNK = 1024
WINDOW = CHUNK + 32
HEAD = 256
HALF = T // 2

FLOPS = 2 * K * S * N
BYTES = K * T * 4 + E * K * N + E * K * N // 32 + N * E * 4 + S * 4 + P * (S + 4 * T) // 8 + N * T * 4

F32 = mybir.dt.float32
BF16 = mybir.dt.bfloat16
I32 = mybir.dt.int32
U32 = mybir.dt.uint32
U16 = mybir.dt.uint16
U8 = mybir.dt.uint8
FP8X4 = mybir.dt.float8_e4m3fn_x4
MULT = mybir.AluOpType.mult
ADD = mybir.AluOpType.add
GELU = mybir.ActivationFunctionType.Gelu_apprx_tanh


def tile_moe_pre_lin_gelu_kernel(tc, xT, w_words, w_scales, b, gate, offs, pos1, pos2, pos3, pos4, out):
    nc = tc.nc
    with ExitStack() as ctx:
        keep = ctx.enter_context(tc.tile_pool(name="keep", bufs=1))
        ring = ctx.enter_context(tc.tile_pool(name="ring", bufs=2))
        psum = ctx.enter_context(tc.psum_pool(name="psum", bufs=8))

        offs_sb = keep.tile([P, S // 16], U16, name="offs_sb")
        pos_sb = [keep.tile([P, T // 16], U16, name="pos_sb%d" % r) for r in range(4)]
        gate_sb = keep.tile([P, S], F32, name="gate_sb")
        bias_sb = keep.tile([P, E], F32, name="bias_sb")
        x_sb = [[keep.tile([P, WINDOW], F32, name="x_sb%d_%d" % (a, t)) for t in range(PACK)] for a in range(PASSES)]
        chunks = S // CHUNK
        per_chunk = CHUNK // C
        w_sb = [keep.tile([P, per_chunk * PASSES, N * PACK], U8, name="w_sb%d" % c, align_bytes=64) for c in range(chunks)]
        ws_sb = keep.tile([P, E * PASSES, N], U8, name="ws_sb", align_bytes=64)
        y_sb = keep.tile([P, S], F32, name="y_sb")

        for a in range(PASSES):
            for t in range(PACK):
                nc.gpsimd.memset(x_sb[a][t][:, T:WINDOW], 0.0)
        nc.gpsimd.memset(ws_sb[:].rearrange("p g n -> p (g n)").bitcast(I32), 0)

        x_rows = xT.rearrange("(a p t) c -> a t p c", p=P, t=PACK)
        nc.sync.dma_start(offs_sb[:], offs)
        nc.scalar.dma_start(x_sb[0][0][:, 0:T], x_rows[0, 0])
        nc.sync.dma_start(gate_sb[:, 0:HEAD], gate[0:P, 0:HEAD])
        nc.sync.dma_start(gate_sb[:, HEAD:CHUNK], gate[0:P, HEAD:CHUNK])
        for a in range(PASSES):
            for t in range(PACK):
                if (a, t) != (0, 0):
                    nc.sync.dma_start(x_sb[a][t][:, 0:T], x_rows[a, t])
        scale_rows = w_scales.rearrange("e a (q r) n -> r q (e a) n", r=4)
        for r in range(4):
            nc.sync.dma_start(ws_sb[r:P:32, :, :].bitcast(I32), scale_rows[r].bitcast(I32))
        for c in range(chunks):
            words = w_words[c * per_chunk : (c + 1) * per_chunk].rearrange("e a p n r -> p (e a) (n r)")
            nc.sync.dma_start(w_sb[c][:].bitcast(I32), words.bitcast(I32))
            if c == 0:
                nc.sync.dma_start(bias_sb[:], b)
                nc.sync.dma_start(gate_sb[:, CHUNK:S], gate[0:P, CHUNK:S])
        for r, pos in enumerate((pos1, pos2, pos3, pos4)):
            nc.sync.dma_start(pos_sb[r][:], pos)

        steps = [(a, c * CHUNK, CHUNK) for c in range(chunks) for a in range(PASSES)]
        last_a, last_s0, last_n = steps.pop()
        steps.extend([(last_a, last_s0, 512), (last_a, last_s0 + 512, 256), (last_a, last_s0 + 768, 256)])

        acc = {}

        def gather(i):
            a, s0, n = steps[i]
            planes = ring.tile([P, PACK, n], F32, name="planes", tag="planes", bufs=3)
            for t in range(PACK):
                cuts = [(0, HEAD), (HEAD, n)] if (i, t) == (0, 0) else [(0, n)]
                for lo, hi in cuts:
                    picked = x_sb[a][t][:].indirect(offs_sb[:, (s0 + lo) // 16 : (s0 + hi) // 16])
                    nc.vector.tensor_tensor(planes[:, t, lo:hi], picked, gate_sb[:, s0 + lo : s0 + hi], MULT)
            return planes

        def weave(i, planes):
            n = steps[i][2]
            grouped = ring.tile([P, n, PACK], BF16, name="grouped", tag="grouped", align_bytes=64)
            if i == len(steps) - 1:
                nc.vector.tensor_copy(grouped[:], planes[:].rearrange("p t s -> p s t"))
            else:
                nc.scalar.copy(grouped[:], planes[:].rearrange("p t s -> p s t"))
            return grouped

        def multiply(i, grouped):
            a, s0, n = steps[i]
            codes = ring.tile([P, n], U32, name="codes", tag="codes", align_bytes=64)
            scales = ring.tile([P, n], U8, name="scales", tag="scales", align_bytes=64)
            nc.vector.quantize_mx(out=codes[:].bitcast(FP8X4), scales=scales[:], in_=grouped[:].rearrange("p s t -> p (s t)"))
            for j in range(n // C):
                e = s0 // C + j
                if a == 0:
                    acc[e] = psum.tile([N, C], F32, name="acc", tag="acc")
                nc.tensor.matmul_mx(
                    out=acc[e][:],
                    lhsT=w_sb[e // per_chunk][:, (e % per_chunk) * PASSES + a, :].bitcast(FP8X4),
                    lhsT_scale=ws_sb[:, e * PASSES + a, :],
                    rhs=codes[:, j * C : (j + 1) * C].bitcast(FP8X4),
                    rhs_scale=scales[:, j * C : (j + 1) * C],
                    start=(a == 0),
                    stop=(a == PASSES - 1),
                )
                if a == PASSES - 1:
                    nc.scalar.activation(y_sb[:, e * C : (e + 1) * C], acc[e][:], GELU, bias=bias_sb[:, e : e + 1])

        waiting = None
        for i in range(len(steps)):
            planes = gather(i)
            if waiting is not None:
                multiply(i - 1, waiting)
            waiting = weave(i, planes)
        multiply(len(steps) - 1, waiting)

        sums = [None, None]
        for r in range(4):
            for h in range(2):
                picked = y_sb[:].indirect(pos_sb[r][:, h * HALF // 16 : (h + 1) * HALF // 16])
                total = ring.tile([P, HALF], F32, name="total", tag="total%d" % h)
                if r == 0:
                    nc.vector.tensor_copy(total[:], picked)
                else:
                    nc.vector.tensor_tensor(total[:], picked, sums[h][:], ADD)
                sums[h] = total
                if r == 3:
                    nc.sync.dma_start(out[:, h * HALF : (h + 1) * HALF], total[:])
